import numpy as np
import ml_dtypes


def mxq(x, axis, fmt="e4m3"):
    dtype, down = {"e4m3": (ml_dtypes.float8_e4m3fn, 7), "e5m2": (ml_dtypes.float8_e5m2, 14)}[fmt]
    v = np.moveaxis(np.asarray(x, np.float32).astype(ml_dtypes.bfloat16).astype(np.float64), axis, -1)
    blocks = v.reshape(v.shape[:-1] + (-1, 32))
    amax = np.abs(blocks).max(-1, keepdims=True)
    byte = np.maximum(np.where(amax > 0, np.frexp(amax)[1] - 1 + 127, 0) - down, 1)
    scale = np.exp2(byte - 127.0)
    codes = (blocks / scale).astype(np.float32).astype(dtype).astype(np.float64)
    return np.moveaxis((codes * scale).reshape(v.shape), -1, axis)


WIDE = False


def mx_kscale(k):
    if not WIDE:
        return np.ones(k)
    levels = np.array([10, -10, 5, -5, 0])
    if k % 512:
        return np.exp2(np.random.permutation(np.resize(levels, k // 32))).repeat(32)
    a = np.empty((k // 512, 16))
    for p in range(k // 512):
        a[p, :8] = np.random.permutation(np.resize(levels, 8))
        for g in range(8):
            far = levels[np.abs(levels - a[p, g]) >= 10]
            a[p, g + 8] = far[np.random.randint(len(far))]
    return np.exp2(a.ravel()).repeat(32)


def f64(x):
    return np.asarray(x).astype(np.float64)


def striped(idx):
    return np.tile(idx.reshape(-1, 16).T, (8, 1)).astype(np.uint16)


def unstriped(offs):
    return offs[:16].T.reshape(-1).astype(np.int64)


E2M1 = np.array([0.0, 0.5, 1.0, 1.5, 2.0, 3.0, 4.0, 6.0, -0.0, -0.5, -1.0, -1.5, -2.0, -3.0, -4.0, -6.0])


def pack_weight(w, fmt):
    k, n = w.shape
    w = f64(np.asarray(w, np.float32).astype(ml_dtypes.bfloat16)).reshape(k // 32, 32, n)
    amax = np.abs(w).max(1)
    if fmt == "e4m3":
        byte = np.frexp(amax)[1] - 1 + 127 - 7
    else:
        mant, ex = np.frexp(amax / 6.0)
        byte = np.where(mant > 0.5, ex, ex - 1) + 127
    byte = np.clip(np.where(amax > 0, byte, 1), 1, 254)
    scaled = (w * np.exp2(127.0 - byte)[:, None, :]).reshape(k, n).astype(np.float32)
    by_word = np.ascontiguousarray(scaled.reshape(k // 512, 128, 4, n).transpose(0, 1, 3, 2))
    if fmt == "e4m3":
        words = by_word.astype(ml_dtypes.float8_e4m3fn).view(np.uint8)
    else:
        c = by_word.astype(ml_dtypes.float4_e2m1fn).view(np.uint8) & 0xF
        words = (c[..., 0::2] | (c[..., 1::2] << 4)).reshape(k // 512, 128, 2 * n)
    return np.ascontiguousarray(words), np.ascontiguousarray(byte.astype(np.uint8).reshape(k // 512, 16, n))


def unpack_weight(words, scales, fmt):
    g, _, n = scales.shape
    words = np.ascontiguousarray(words).reshape(g, 128, n, -1)
    if fmt == "e4m3":
        vals = words.view(ml_dtypes.float8_e4m3fn).astype(np.float64)
    else:
        nib = np.empty((g, 128, n, 4), np.uint8)
        nib[..., 0::2] = words & 0xF
        nib[..., 1::2] = words >> 4
        vals = E2M1[nib]
    vals = vals * np.repeat(np.exp2(scales.astype(np.float64) - 127.0), 8, axis=1)[..., None]
    return vals.transpose(0, 1, 3, 2).reshape(g * 512, n)


def gelu(v):
    return 0.5 * v * (1.0 + np.tanh(np.sqrt(2.0 / np.pi) * (v + 0.044715 * v**3)))


def bf(x):
    return np.asarray(x, np.float32).astype(ml_dtypes.bfloat16)


def planes(Y):
    n, m = Y.shape
    b = f64(bf(Y)).reshape(n // 32, 32, m)
    amax = np.abs(b).max(1)
    byte = np.clip(np.where(amax > 0, np.frexp(amax)[1] - 1 + 127 - 7, 1), 1, 254)
    codes = (b * np.exp2(127.0 - byte)[:, None, :]).reshape(n, m).astype(np.float32).astype(ml_dtypes.float8_e4m3fn).view(np.uint8)
    words = codes.reshape(n // 512, 128, 4, m).transpose(0, 1, 3, 2)
    return np.ascontiguousarray(words), np.ascontiguousarray(byte.astype(np.uint8).reshape(n // 512, 16, m))


K, M, H, N, T, S, T2, P = 1024, 512, 1024, 512, 4096, 1024, 1024, 512


def setup_inputs():
    n = np.random.standard_normal
    s = mx_kscale(K)[:, None]
    s2 = mx_kscale(M)[:, None]
    u = mx_kscale(H)[:, None]
    size = np.exp(0.8 * n(N))[None, :]
    tab_words, tab_scales = pack_weight(n((K, T)) * s, "e4m3")
    tab2_words, tab2_scales = pack_weight(n((M, T2)) * s2, "e4m3")
    w1 = 1.4 * n((K, H)) / np.sqrt(K) / s
    w2_words, w2_scales = pack_weight(n((H, N)) / np.sqrt(H) / u * size, "e2m1")
    w3 = n((K, N)) / np.sqrt(K) / s * size
    w4_words, w4_scales = pack_weight(0.8 * n((M, N)) / np.sqrt(M) / s2 * size, "e4m3")
    return {
        "tab_words": tab_words, "tab_scales": tab_scales,
        "offs": striped(np.random.permutation(T)[:S]),
        "tab2_words": tab2_words, "tab2_scales": tab2_scales,
        "offs2": striped(np.random.permutation(T2)[:P]),
        "pos1": striped(np.random.permutation(S)[:P]),
        "w1": w1.astype(np.float32),
        "gain": (np.exp(0.3 * n(H)) * u[:, 0]).astype(np.float32),
        "shift": (0.5 * n(H) * u[:, 0]).astype(np.float32),
        "w2_words": w2_words, "w2_scales": w2_scales,
        "w3": w3.astype(np.float32),
        "w4_words": w4_words, "w4_scales": w4_scales,
    }


def reference(tab_words, tab_scales, offs, tab2_words, tab2_scales, offs2, pos1, w1, gain, shift, w2_words, w2_scales, w3, w4_words, w4_scales):
    v = unpack_weight(tab_words, tab_scales, "e4m3")[:, unstriped(offs)]
    v2 = unpack_weight(tab2_words, tab2_scales, "e4m3")[:, unstriped(offs2)]
    w2 = unpack_weight(w2_words, w2_scales, "e2m1")
    w4 = unpack_weight(w4_words, w4_scales, "e4m3")
    a = mxq(f64(w1), 0, "e4m3").T @ v
    h = f64(gain)[:, None] * np.tanh(a) + f64(shift)[:, None]
    d = w2.T @ mxq(h, 0, "e4m3")
    skip = mxq(f64(w3), 0, "e4m3").T @ v
    d = np.maximum(d, skip)
    b = w4.T @ v2
    y = d[:, unstriped(pos1)] + b
    words, scales = planes(y)
    return y, words, scales

@@ -1,0 +1,252 @@
+from contextlib import ExitStack
+
+import concourse.mybir as mybir
+
+K, M, H, N, T, S, T2, PICK = 1024, 512, 1024, 512, 4096, 1024, 1024, 512
+FLOPS = 2 * (K * H * S + H * N * S + K * N * S + M * N * PICK)
+
+F32 = mybir.dt.float32
+BF16 = mybir.dt.bfloat16
+I32 = mybir.dt.int32
+U32 = mybir.dt.uint32
+U16 = mybir.dt.uint16
+U8 = mybir.dt.uint8
+FP8X4 = mybir.dt.float8_e4m3fn_x4
+FP4X4 = mybir.dt.float4_e2m1fn_x4
+ACT = mybir.ActivationFunctionType
+ALU = mybir.AluOpType
+
+P = 128
+PACK = 4
+PASS = P * PACK
+BANK = 512
+
+
+def tile_list_migraine_trigger_scores_kernel(
+    tc, tab_words, tab_scales, offs, tab2_words, tab2_scales, offs2, pos1, w1, gain, shift,
+    w2_words, w2_scales, w3, w4_words, w4_scales, out_0, out_1, out_2,
+):
+    nc = tc.nc
+    with ExitStack() as ctx:
+        keep = ctx.enter_context(tc.tile_pool(name="keep", bufs=1))
+        ring = ctx.enter_context(tc.tile_pool(name="ring", bufs=2))
+        psum = ctx.enter_context(tc.psum_pool(name="psum", bufs=1))
+
+        def held(name, shape, dtype):
+            return keep.tile(shape, dtype, name=name, align_bytes=64)
+
+        def as_words(dram_words):
+            return dram_words.rearrange("p c i -> p (c i)").bitcast(I32)
+
+        offs_sb = held("offs_sb", [P, S // 16], U16)
+        offs2_sb = held("offs2_sb", [P, PICK // 16], U16)
+        pos1_sb = held("pos1_sb", [P, PICK // 16], U16)
+        tab_s = held("tab_s", [P, T], U8)
+        tab2_s = held("tab2_s", [P, T2], U8)
+        w2_w = held("w2_w", [P, 2, 2 * N], U8)
+        w2_s = held("w2_s", [P, 2, N], U8)
+        w4_s = held("w4_s", [P, N], U8)
+        gain_sb = held("gain_sb", [P, 2, PACK], F32)
+        shift_sb = held("shift_sb", [P, 2, PACK], F32)
+
+        for plane in (tab2_s, w4_s, tab_s):
+            nc.vector.memset(plane[:].bitcast(I32), 0)
+        nc.vector.memset(w2_s[:].rearrange("p a c -> p (a c)").bitcast(I32), 0)
+
+        def weight_rows(w, a, c0):
+            return w[a * PASS : (a + 1) * PASS, c0 : c0 + PASS].rearrange("(p j) c -> p j c", j=PACK)
+
+        def load_w1(a, b):
+            raw = ring.tile([P, PACK, PASS], F32, name="raw", bufs=2, align_bytes=64)
+            nc.sync.dma_start(out=raw[:], in_=weight_rows(w1, a, b * PASS))
+            return raw
+
+        def wide(name, shape, dtype):
+            return ring.tile(shape, dtype, name=name, tag="wide", bufs=2, align_bytes=64)
+
+        tab2_w = wide("tab2_w", [P, T2], I32)
+        w4_w = wide("w4_w", [P, N], I32)
+        nc.sync.dma_start(offs2_sb[:], offs2)
+        nc.sync.dma_start(out=tab2_w[:], in_=as_words(tab2_words[0]))
+        nc.sync.dma_start(out=w4_w[:], in_=as_words(w4_words[0]))
+        nc.sync.dma_start(out=w2_w[:].bitcast(I32), in_=w2_words.rearrange("a p c -> p a c").bitcast(I32))
+        nc.sync.dma_start(offs_sb[:], offs)
+        nc.sync.dma_start(pos1_sb[:], pos1)
+        w1_raw = {(a, 0): load_w1(a, 0) for a in range(2)}
+        for q in range(4):
+            nc.scalar.dma_start(out=tab2_s[32 * q : 32 * q + 4, :].bitcast(I32), in_=tab2_scales[0, 4 * q : 4 * q + 4, :].bitcast(I32))
+        for q in range(4):
+            nc.scalar.dma_start(out=tab_s[32 * q : 32 * q + 8, :].bitcast(I32), in_=tab_scales[:, 4 * q : 4 * q + 4, :].bitcast(I32))
+        nc.gpsimd.dma_start(out=gain_sb[:], in_=gain.rearrange("(b p t) -> p b t", b=2, t=PACK))
+        nc.gpsimd.dma_start(out=shift_sb[:], in_=shift.rearrange("(b p t) -> p b t", b=2, t=PACK))
+        for q in range(4):
+            nc.gpsimd.dma_start(out=w4_s[32 * q : 32 * q + 4, :].bitcast(I32), in_=w4_scales[0, 4 * q : 4 * q + 4, :].bitcast(I32))
+        for q in range(4):
+            nc.gpsimd.dma_start(
+                out=w2_s[32 * q : 32 * q + 4, :, :].bitcast(I32),
+                in_=w2_scales[:, 4 * q : 4 * q + 4, :].rearrange("a r c -> r a c").bitcast(I32),
+            )
+
+        def round_weight(raw, on_scalar):
+            grouped = ring.tile([P, PACK * PASS], BF16, name="grouped", bufs=3, align_bytes=64)
+            dst = grouped[:].rearrange("p (t m j) -> p m j t", t=PACK, j=PACK)
+            src = raw.rearrange("p j (m t) -> p m j t", t=PACK)
+            if on_scalar:
+                nc.scalar.copy(out=dst, in_=src)
+            else:
+                nc.vector.tensor_copy(out=dst, in_=src)
+            return grouped
+
+        def quantise(name, grouped, cols):
+            codes = held(name + "_codes", [P, cols], U32)
+            scales = held(name + "_scales", [P, cols], U8)
+            nc.vector.quantize_mx(out=codes[:].bitcast(FP8X4), scales=scales[:], in_=grouped[:])
+            return codes, scales
+
+        def weave(dst, src, on_scalar):
+            dst = dst.rearrange("p (c i t) -> p c t i", t=PACK, i=4)
+            src = src.rearrange("p t (c i) -> p c t i", i=4)
+            if on_scalar:
+                nc.scalar.copy(out=dst, in_=src)
+            else:
+                nc.vector.tensor_copy(out=dst, in_=src)
+
+        def bank():
+            return psum.tile([P, BANK], F32, name="bank", bufs=8)
+
+        def cols(t, width=P):
+            return slice(t * width, (t + 1) * width)
+
+        v2_w = held("v2_w", [P, PICK], U32)
+        v2_s = held("v2_s", [P, PICK], U8)
+        w4d_w = held("w4d_w", [P, N], I32)
+        w4d_s = held("w4d_s", [P, N], U8)
+        w2d_w = held("w2d_w", [P, 2, PACK, 2 * P], U8)
+        w2d_s = held("w2d_s", [P, 2, PACK, P], U8)
+        nc.vector.tensor_copy(out=v2_w[:], in_=tab2_w[:].bitcast(U32).indirect(offs2_sb[:]))
+        nc.vector.tensor_copy(out=w4d_w[:].rearrange("p (t m) -> p m t", t=PACK), in_=w4_w[:].rearrange("p (m t) -> p m t", t=PACK))
+        tab_w = []
+        for a in range(2):
+            tab_w.append(wide("tab_w%d" % a, [P, T], I32))
+            nc.sync.dma_start(out=tab_w[a][:], in_=as_words(tab_words[a]))
+        nc.vector.tensor_copy(
+            out=w2d_w[:].rearrange("p a t (m e) -> p a m t e", e=2),
+            in_=w2_w[:].rearrange("p a (m t e) -> p a m t e", t=PACK, e=2),
+        )
+        nc.vector.tensor_copy(out=v2_s[:], in_=tab2_s[:].indirect(offs2_sb[:]))
+        nc.vector.tensor_copy(out=w4d_s[:].rearrange("p (t m) -> p m t", t=PACK), in_=w4_s[:].rearrange("p (m t) -> p m t", t=PACK))
+        v_w = [held("v_w%d" % a, [P, S], U32) for a in range(2)]
+        v_s = held("v_s", [P, S], U8)
+        nc.vector.tensor_copy(out=v_s[:], in_=tab_s[:].indirect(offs_sb[:]))
+
+        w1_q = {}
+        for a in range(2):
+            w1_q[(a, 0)] = quantise("w1_%d0" % a, round_weight(w1_raw[(a, 0)][:], True), PASS)
+            w1_raw[(a, 1)] = load_w1(a, 1)
+
+        expo = []
+        for t in range(PACK):
+            acc = bank()
+            nc.tensor.matmul_mx(
+                out=acc[:], lhsT=w4d_w[:, cols(t)].bitcast(FP8X4), lhsT_scale=w4d_s[:, cols(t)],
+                rhs=v2_w[:].bitcast(FP8X4), rhs_scale=v2_s[:], start=True, stop=True,
+            )
+            expo_t = held("expo%d" % t, [P, PICK], F32)
+            nc.scalar.copy(out=expo_t[:], in_=acc[:])
+            expo.append(expo_t)
+
+        nc.vector.tensor_copy(out=v_w[0][:], in_=tab_w[0][:].bitcast(U32).indirect(offs_sb[:]))
+        w3_raw = wide("w3_raw", [P, 2, PACK, N], F32)
+        for a in range(2):
+            nc.sync.dma_start(out=w3_raw[:, a], in_=weight_rows(w3, a, 0))
+        nc.vector.tensor_copy(
+            out=w2d_s[:].rearrange("p a t m -> p a m t"),
+            in_=w2_s[:].rearrange("p a (m t) -> p a m t", t=PACK),
+        )
+        for half in range(2):
+            nc.vector.tensor_copy(
+                out=v_w[1][:, cols(half, BANK)],
+                in_=tab_w[1][:].bitcast(U32).indirect(offs_sb[:, cols(half, BANK // 16)]),
+            )
+
+        def times_table(weight, t, half):
+            acc = bank()
+            for a in range(2):
+                codes, scales = weight[a]
+                nc.tensor.matmul_mx(
+                    out=acc[:], lhsT=codes[:, cols(t)].bitcast(FP8X4), lhsT_scale=scales[:, cols(t)],
+                    rhs=v_w[a][:, cols(half, BANK)].bitcast(FP8X4), rhs_scale=v_s[4 * a : P, cols(half, BANK)],
+                    start=(a == 0), stop=(a == 1),
+                )
+            return acc
+
+        def features(b, half):
+            rounded = ring.tile([P, PACK, BANK], BF16, name="rounded", bufs=2, align_bytes=64)
+            for t in range(PACK):
+                acc = times_table([w1_q[(0, b)], w1_q[(1, b)]], t, half)
+                bent = ring.tile([P, BANK], F32, name="bent", bufs=6, align_bytes=64)
+                nc.scalar.activation(out=bent[:], in_=acc[:], func=ACT.Tanh)
+                gain_t, shift_t = gain_sb[:, b, t : t + 1], shift_sb[:, b, t : t + 1]
+                if half == 1:
+                    nc.scalar.activation(out=rounded[:, t, :], in_=bent[:], func=ACT.Identity, scale=gain_t, bias=shift_t)
+                else:
+                    nc.vector.tensor_scalar(
+                        out=rounded[:, t, :], in0=bent[:], scalar1=gain_t, scalar2=shift_t, op0=ALU.mult, op1=ALU.add
+                    )
+            woven = ring.tile([P, PACK * BANK], BF16, name="woven", bufs=2, align_bytes=64)
+            weave(woven[:], rounded[:], (b, half) == (0, 0))
+            return quantise("h_%d%d" % (b, half), woven, BANK)
+
+        day = [held("day%d" % t, [P, S], F32) for t in range(PACK)]
+
+        def straight(half):
+            for t in range(PACK):
+                acc = times_table(w3_q, t, half)
+                nc.scalar.copy(out=day[t][:, cols(half, BANK)], in_=acc[:])
+
+        def second_stage(half):
+            for t in range(PACK):
+                acc = bank()
+                for b in range(2):
+                    codes, scales = h_q[(b, half)]
+                    nc.tensor.matmul_mx(
+                        out=acc[:], lhsT=w2d_w[:, b, t, :].bitcast(FP4X4), lhsT_scale=w2d_s[:, b, t, :],
+                        rhs=codes[:].bitcast(FP8X4), rhs_scale=scales[:], start=(b == 0), stop=(b == 1),
+                    )
+                here = day[t][:, cols(half, BANK)]
+                nc.vector.tensor_tensor(out=here, in0=acc[:], in1=here, op=ALU.max)
+
+        h_q = {}
+        h_q[(0, 0)] = features(0, 0)
+        w1_q[(0, 1)] = quantise("w1_01", round_weight(w1_raw[(0, 1)][:], False), PASS)
+        h_q[(0, 1)] = features(0, 1)
+        w1_q[(1, 1)] = quantise("w1_11", round_weight(w1_raw[(1, 1)][:], False), PASS)
+        h_q[(1, 0)] = features(1, 0)
+        w3_q = [quantise("w3_%d" % a, round_weight(w3_raw[:, a], False), PASS) for a in range(2)]
+        h_q[(1, 1)] = features(1, 1)
+        straight(0)
+        second_stage(0)
+        straight(1)
+        second_stage(1)
+
+        out_rows = out_0.rearrange("(p t) j -> p t j", t=PACK)
+        out_words = as_words(out_1[0])
+        y_codes = held("y_codes", [P, PICK], U32)
+        y_scales = held("y_scales", [P, PICK], U8)
+        width = PICK // 2
+        for half in range(2):
+            js = cols(half, width)
+            y = held("y%d" % half, [P, PACK, width], F32)
+            for t in range(PACK):
+                nc.vector.tensor_tensor(
+                    out=y[:, t, :], in0=day[t][:].indirect(pos1_sb[:, cols(half, width // 16)]), in1=expo[t][:, js], op=ALU.add
+                )
+                if t % 2 == 1:
+                    nc.sync.dma_start(out=out_rows[:, t - 1 : t + 1, js], in_=y[:, t - 1 : t + 1, :])
+            y_woven = held("y_woven%d" % half, [P, PACK * width], BF16)
+            weave(y_woven[:], y[:], half == 0)
+            nc.vector.quantize_mx(out=y_codes[:, js].bitcast(FP8X4), scales=y_scales[:, js], in_=y_woven[:])
+            nc.sync.dma_start(out=out_words[:, js], in_=y_codes[:, js].bitcast(I32))
+        for q in range(4):
+            queue = nc.scalar if q % 2 else nc.sync
+            queue.dma_start(out=out_2[0, 4 * q : 4 * q + 4, :].bitcast(I32), in_=y_scales[32 * q : 32 * q + 4, :].bitcast(I32))

@@ -41,51 +41,36 @@ def tile_list_migraine_trigger_scores_kernel(
         offs_sb = held("offs_sb", [P, S // 16], U16)
         offs2_sb = held("offs2_sb", [P, PICK // 16], U16)
         pos1_sb = held("pos1_sb", [P, PICK // 16], U16)
-        tab_s = held("tab_s", [P, T], U8)
-        tab2_s = held("tab2_s", [P, T2], U8)
-        w2_w = held("w2_w", [P, 2, 2 * N], U8)
-        w2_s = held("w2_s", [P, 2, N], U8)
-        w4_s = held("w4_s", [P, N], U8)
-        gain_sb = held("gain_sb", [P, 2, PACK], F32)
-        shift_sb = held("shift_sb", [P, 2, PACK], F32)
 
-        for plane in (tab2_s, w4_s, tab_s):
-            nc.vector.memset(plane[:].bitcast(I32), 0)
-        nc.vector.memset(w2_s[:].rearrange("p a c -> p (a c)").bitcast(I32), 0)
+        def slot(tag, name, shape, dtype):
+            return ring.tile(shape, dtype, name=name, tag=tag, bufs=1, align_bytes=64)
 
-        def weight_rows(w, a, c0):
-            return w[a * PASS : (a + 1) * PASS, c0 : c0 + PASS].rearrange("(p j) c -> p j c", j=PACK)
-
-        def load_w1(a, b):
-            raw = ring.tile([P, PACK, PASS], F32, name="raw", bufs=2, align_bytes=64)
-            nc.sync.dma_start(out=raw[:], in_=weight_rows(w1, a, b * PASS))
+        def load_weight(raw, w, a, c0):
+            rows = w[a * PASS : (a + 1) * PASS, c0 : c0 + PASS]
+            nc.sync.dma_start(out=raw, in_=rows.rearrange("(p j) c -> p j c", j=PACK))
             return raw
 
-        def wide(name, shape, dtype):
-            return ring.tile(shape, dtype, name=name, tag="wide", bufs=2, align_bytes=64)
+        def load_plane(queue, plane, rows, dram_rows):
+            for q in range(4):
+                queue.dma_start(out=plane[32 * q : 32 * q + rows].bitcast(I32), in_=dram_rows(slice(4 * q, 4 * q + 4)).bitcast(I32))
 
-        tab2_w = wide("tab2_w", [P, T2], I32)
-        w4_w = wide("w4_w", [P, N], I32)
+        RAW = [P, PACK, PASS]
+
+        tab2_w = slot("slot_a", "tab2_w", [P, T2], I32)
+        w4_w = slot("slot_b", "w4_w", [P, N], I32)
+        w2_w = slot("slot_c", "w2_w", [P, 2, 2 * N], U8)
+        tab_s = slot("slot_d", "tab_s", [P, T], U8)
+        nc.vector.memset(tab_s[:].bitcast(I32), 0)
         nc.sync.dma_start(offs2_sb[:], offs2)
         nc.sync.dma_start(out=tab2_w[:], in_=as_words(tab2_words[0]))
         nc.sync.dma_start(out=w4_w[:], in_=as_words(w4_words[0]))
         nc.sync.dma_start(out=w2_w[:].bitcast(I32), in_=w2_words.rearrange("a p c -> p a c").bitcast(I32))
         nc.sync.dma_start(offs_sb[:], offs)
         nc.sync.dma_start(pos1_sb[:], pos1)
-        w1_raw = {(a, 0): load_w1(a, 0) for a in range(2)}
-        for q in range(4):
-            nc.scalar.dma_start(out=tab2_s[32 * q : 32 * q + 4, :].bitcast(I32), in_=tab2_scales[0, 4 * q : 4 * q + 4, :].bitcast(I32))
-        for q in range(4):
-            nc.scalar.dma_start(out=tab_s[32 * q : 32 * q + 8, :].bitcast(I32), in_=tab_scales[:, 4 * q : 4 * q + 4, :].bitcast(I32))
-        nc.gpsimd.dma_start(out=gain_sb[:], in_=gain.rearrange("(b p t) -> p b t", b=2, t=PACK))
-        nc.gpsimd.dma_start(out=shift_sb[:], in_=shift.rearrange("(b p t) -> p b t", b=2, t=PACK))
-        for q in range(4):
-            nc.gpsimd.dma_start(out=w4_s[32 * q : 32 * q + 4, :].bitcast(I32), in_=w4_scales[0, 4 * q : 4 * q + 4, :].bitcast(I32))
-        for q in range(4):
-            nc.gpsimd.dma_start(
-                out=w2_s[32 * q : 32 * q + 4, :, :].bitcast(I32),
-                in_=w2_scales[:, 4 * q : 4 * q + 4, :].rearrange("a r c -> r a c").bitcast(I32),
-            )
+        w1_raw = {}
+        for a, tag in enumerate(("slot_e", "slot_f")):
+            w1_raw[(a, 0)] = load_weight(slot(tag, "w1_raw%d0" % a, RAW, F32)[:], w1, a, 0)
+        load_plane(nc.sync, tab_s, 8, lambda r: tab_scales[:, r, :])
 
         def round_weight(raw, on_scalar):
             grouped = ring.tile([P, PACK * PASS], BF16, name="grouped", bufs=3, align_bytes=64)
@@ -111,8 +96,8 @@ def tile_list_migraine_trigger_scores_kernel(
             else:
                 nc.vector.tensor_copy(out=dst, in_=src)
 
-        def bank():
-            return psum.tile([P, BANK], F32, name="bank", bufs=8)
+        def bank(tag):
+            return psum.tile([P, BANK], F32, name=tag, bufs=3 if tag == "first" else 5)
 
         def cols(t, width=P):
             return slice(t * width, (t + 1) * width)
@@ -120,57 +105,49 @@ def tile_list_migraine_trigger_scores_kernel(
         v2_w = held("v2_w", [P, PICK], U32)
         v2_s = held("v2_s", [P, PICK], U8)
         w4d_w = held("w4d_w", [P, N], I32)
-        w4d_s = held("w4d_s", [P, N], U8)
         w2d_w = held("w2d_w", [P, 2, PACK, 2 * P], U8)
-        w2d_s = held("w2d_s", [P, 2, PACK, P], U8)
         nc.vector.tensor_copy(out=v2_w[:], in_=tab2_w[:].bitcast(U32).indirect(offs2_sb[:]))
+        tab_w = [slot("slot_a", "tab_w0", [P, T], I32)]
+        nc.sync.dma_start(out=tab_w[0][:], in_=as_words(tab_words[0]))
         nc.vector.tensor_copy(out=w4d_w[:].rearrange("p (t m) -> p m t", t=PACK), in_=w4_w[:].rearrange("p (m t) -> p m t", t=PACK))
-        tab_w = []
-        for a in range(2):
-            tab_w.append(wide("tab_w%d" % a, [P, T], I32))
-            nc.sync.dma_start(out=tab_w[a][:], in_=as_words(tab_words[a]))
+        tab2_s = slot("slot_b", "tab2_s", [P, T2], U8)
+        nc.vector.memset(tab2_s[:].bitcast(I32), 0)
+        load_plane(nc.sync, tab2_s, 4, lambda r: tab2_scales[0, r, :])
         nc.vector.tensor_copy(
             out=w2d_w[:].rearrange("p a t (m e) -> p a m t e", e=2),
             in_=w2_w[:].rearrange("p a (m t e) -> p a m t e", t=PACK, e=2),
         )
-        nc.vector.tensor_copy(out=v2_s[:], in_=tab2_s[:].indirect(offs2_sb[:]))
-        nc.vector.tensor_copy(out=w4d_s[:].rearrange("p (t m) -> p m t", t=PACK), in_=w4_s[:].rearrange("p (m t) -> p m t", t=PACK))
+        affine = slot("slot_c", "affine", [P, 2, 2, PACK], F32)
+        gain_sb, shift_sb = affine[:, 0], affine[:, 1]
+        nc.sync.dma_start(out=gain_sb, in_=gain.rearrange("(b p t) -> p b t", b=2, t=PACK))
+        nc.sync.dma_start(out=shift_sb, in_=shift.rearrange("(b p t) -> p b t", b=2, t=PACK))
+
         v_w = [held("v_w%d" % a, [P, S], U32) for a in range(2)]
         v_s = held("v_s", [P, S], U8)
         nc.vector.tensor_copy(out=v_s[:], in_=tab_s[:].indirect(offs_sb[:]))
-
-        w1_q = {}
+        w1_q = {(0, 0): quantise("w1_00", round_weight(w1_raw[(0, 0)], True), PASS)}
+        tab_w.append(slot("slot_e", "tab_w1", [P, T], I32))
+        nc.sync.dma_start(out=tab_w[1][:], in_=as_words(tab_words[1]))
+        w1_q[(1, 0)] = quantise("w1_10", round_weight(w1_raw[(1, 0)], True), PASS)
+        late_raw = slot("slot_f", "late_raw", [P, 4, PACK, PASS], F32)
         for a in range(2):
-            w1_q[(a, 0)] = quantise("w1_%d0" % a, round_weight(w1_raw[(a, 0)][:], True), PASS)
-            w1_raw[(a, 1)] = load_w1(a, 1)
-
-        expo = []
-        for t in range(PACK):
-            acc = bank()
-            nc.tensor.matmul_mx(
-                out=acc[:], lhsT=w4d_w[:, cols(t)].bitcast(FP8X4), lhsT_scale=w4d_s[:, cols(t)],
-                rhs=v2_w[:].bitcast(FP8X4), rhs_scale=v2_s[:], start=True, stop=True,
-            )
-            expo_t = held("expo%d" % t, [P, PICK], F32)
-            nc.scalar.copy(out=expo_t[:], in_=acc[:])
-            expo.append(expo_t)
+            w1_raw[(a, 1)] = load_weight(late_raw[:, a], w1, a, PASS)
+        w3_raw = [load_weight(late_raw[:, 2 + a], w3, a, 0) for a in range(2)]
 
         nc.vector.tensor_copy(out=v_w[0][:], in_=tab_w[0][:].bitcast(U32).indirect(offs_sb[:]))
-        w3_raw = wide("w3_raw", [P, 2, PACK, N], F32)
-        for a in range(2):
-            nc.sync.dma_start(out=w3_raw[:, a], in_=weight_rows(w3, a, 0))
-        nc.vector.tensor_copy(
-            out=w2d_s[:].rearrange("p a t m -> p a m t"),
-            in_=w2_s[:].rearrange("p a (m t) -> p a m t", t=PACK),
-        )
+        w_s = slot("slot_a", "w_s", [P, 3, N], U8)
+        nc.vector.memset(w_s[:].rearrange("p a c -> p (a c)").bitcast(I32), 0)
+        load_plane(nc.sync, w_s[:, 0:2], 4, lambda r: w2_scales[:, r, :].rearrange("a r c -> r a c"))
+        load_plane(nc.sync, w_s[:, 2], 4, lambda r: w4_scales[0, r, :])
+        nc.vector.tensor_copy(out=v2_s[:], in_=tab2_s[:].indirect(offs2_sb[:]))
         for half in range(2):
             nc.vector.tensor_copy(
                 out=v_w[1][:, cols(half, BANK)],
                 in_=tab_w[1][:].bitcast(U32).indirect(offs_sb[:, cols(half, BANK // 16)]),
             )
 
-        def times_table(weight, t, half):
-            acc = bank()
+        def times_table(tag, weight, t, half):
+            acc = bank(tag)
             for a in range(2):
                 codes, scales = weight[a]
                 nc.tensor.matmul_mx(
@@ -183,11 +160,11 @@ def tile_list_migraine_trigger_scores_kernel(
         def features(b, half):
             rounded = ring.tile([P, PACK, BANK], BF16, name="rounded", bufs=2, align_bytes=64)
             for t in range(PACK):
-                acc = times_table([w1_q[(0, b)], w1_q[(1, b)]], t, half)
+                acc = times_table("first", [w1_q[(0, b)], w1_q[(1, b)]], t, half)
                 bent = ring.tile([P, BANK], F32, name="bent", bufs=6, align_bytes=64)
                 nc.scalar.activation(out=bent[:], in_=acc[:], func=ACT.Tanh)
                 gain_t, shift_t = gain_sb[:, b, t : t + 1], shift_sb[:, b, t : t + 1]
-                if half == 1:
+                if b != half:
                     nc.scalar.activation(out=rounded[:, t, :], in_=bent[:], func=ACT.Identity, scale=gain_t, bias=shift_t)
                 else:
                     nc.vector.tensor_scalar(
@@ -201,16 +178,16 @@ def tile_list_migraine_trigger_scores_kernel(
 
         def straight(half):
             for t in range(PACK):
-                acc = times_table(w3_q, t, half)
+                acc = times_table("later", w3_q, t, half)
                 nc.scalar.copy(out=day[t][:, cols(half, BANK)], in_=acc[:])
 
         def second_stage(half):
             for t in range(PACK):
-                acc = bank()
+                acc = bank("later")
                 for b in range(2):
                     codes, scales = h_q[(b, half)]
                     nc.tensor.matmul_mx(
-                        out=acc[:], lhsT=w2d_w[:, b, t, :].bitcast(FP4X4), lhsT_scale=w2d_s[:, b, t, :],
+                        out=acc[:], lhsT=w2d_w[:, b, t, :].bitcast(FP4X4), lhsT_scale=wd_s[:, b, t, :],
                         rhs=codes[:].bitcast(FP8X4), rhs_scale=scales[:], start=(b == 0), stop=(b == 1),
                     )
                 here = day[t][:, cols(half, BANK)]
@@ -218,33 +195,47 @@ def tile_list_migraine_trigger_scores_kernel(
 
         h_q = {}
         h_q[(0, 0)] = features(0, 0)
-        w1_q[(0, 1)] = quantise("w1_01", round_weight(w1_raw[(0, 1)][:], False), PASS)
+        w1_q[(0, 1)] = quantise("w1_01", round_weight(w1_raw[(0, 1)], False), PASS)
         h_q[(0, 1)] = features(0, 1)
-        w1_q[(1, 1)] = quantise("w1_11", round_weight(w1_raw[(1, 1)][:], False), PASS)
+        w1_q[(1, 1)] = quantise("w1_11", round_weight(w1_raw[(1, 1)], False), PASS)
         h_q[(1, 0)] = features(1, 0)
-        w3_q = [quantise("w3_%d" % a, round_weight(w3_raw[:, a], False), PASS) for a in range(2)]
+        w3_q = [quantise("w3_%d" % a, round_weight(w3_raw[a], False), PASS) for a in range(2)]
+        wd_s = slot("slot_f", "wd_s", [P, 3, PACK, P], U8)
+        nc.vector.tensor_copy(
+            out=wd_s[:].rearrange("p a t m -> p a m t"),
+            in_=w_s[:].rearrange("p a (m t) -> p a m t", t=PACK),
+        )
         h_q[(1, 1)] = features(1, 1)
         straight(0)
         second_stage(0)
         straight(1)
         second_stage(1)
 
+        expo = []
+        for t in range(PACK):
+            acc = bank("first")
+            nc.tensor.matmul_mx(
+                out=acc[:], lhsT=w4d_w[:, cols(t)].bitcast(FP8X4), lhsT_scale=wd_s[:, 2, t, :],
+                rhs=v2_w[:].bitcast(FP8X4), rhs_scale=v2_s[:], start=True, stop=True,
+            )
+            expo_t = held("expo%d" % t, [P, PICK], F32)
+            nc.scalar.copy(out=expo_t[:], in_=acc[:])
+            expo.append(expo_t)
+
         out_rows = out_0.rearrange("(p t) j -> p t j", t=PACK)
         out_words = as_words(out_1[0])
         y_codes = held("y_codes", [P, PICK], U32)
         y_scales = held("y_scales", [P, PICK], U8)
-        width = PICK // 2
-        for half in range(2):
-            js = cols(half, width)
+        for half, (j0, width) in enumerate(((0, 256), (256, 128), (384, 128))):
+            js = slice(j0, j0 + width)
             y = held("y%d" % half, [P, PACK, width], F32)
             for t in range(PACK):
                 nc.vector.tensor_tensor(
-                    out=y[:, t, :], in0=day[t][:].indirect(pos1_sb[:, cols(half, width // 16)]), in1=expo[t][:, js], op=ALU.add
+                    out=y[:, t, :], in0=day[t][:].indirect(pos1_sb[:, j0 // 16 : (j0 + width) // 16]), in1=expo[t][:, js], op=ALU.add
                 )
-                if t % 2 == 1:
-                    nc.sync.dma_start(out=out_rows[:, t - 1 : t + 1, js], in_=y[:, t - 1 : t + 1, :])
+            nc.sync.dma_start(out=out_rows[:, :, js], in_=y[:])
             y_woven = held("y_woven%d" % half, [P, PACK * width], BF16)
-            weave(y_woven[:], y[:], half == 0)
+            weave(y_woven[:], y[:], half < 2)
             nc.vector.quantize_mx(out=y_codes[:, js].bitcast(FP8X4), scales=y_scales[:, js], in_=y_woven[:])
             nc.sync.dma_start(out=out_words[:, js], in_=y_codes[:, js].bitcast(I32))
         for q in range(4):

from contextlib import ExitStack

import concourse.mybir as mybir

K, M, H, N, T, S, T2, PICK = 1024, 512, 1024, 512, 4096, 1024, 1024, 512
FLOPS = 2 * (K * H * S + H * N * S + K * N * S + M * N * PICK)

F32 = mybir.dt.float32
BF16 = mybir.dt.bfloat16
I32 = mybir.dt.int32
U32 = mybir.dt.uint32
U16 = mybir.dt.uint16
U8 = mybir.dt.uint8
FP8X4 = mybir.dt.float8_e4m3fn_x4
FP4X4 = mybir.dt.float4_e2m1fn_x4
ACT = mybir.ActivationFunctionType
ALU = mybir.AluOpType

P = 128
PACK = 4
PASS = P * PACK
BANK = 512


def tile_list_migraine_trigger_scores_kernel(
    tc, tab_words, tab_scales, offs, tab2_words, tab2_scales, offs2, pos1, w1, gain, shift,
    w2_words, w2_scales, w3, w4_words, w4_scales, out_0, out_1, out_2,
):
    nc = tc.nc
    with ExitStack() as ctx:
        keep = ctx.enter_context(tc.tile_pool(name="keep", bufs=1))
        ring = ctx.enter_context(tc.tile_pool(name="ring", bufs=2))
        psum = ctx.enter_context(tc.psum_pool(name="psum", bufs=1))

        def held(name, shape, dtype):
            return keep.tile(shape, dtype, name=name, align_bytes=64)

        def as_words(dram_words):
            return dram_words.rearrange("p c i -> p (c i)").bitcast(I32)

        offs_sb = held("offs_sb", [P, S // 16], U16)
        offs2_sb = held("offs2_sb", [P, PICK // 16], U16)
        pos1_sb = held("pos1_sb", [P, PICK // 16], U16)

        def slot(tag, name, shape, dtype):
            return ring.tile(shape, dtype, name=name, tag=tag, bufs=1, align_bytes=64)

        def load_weight(raw, w, a, c0):
            rows = w[a * PASS : (a + 1) * PASS, c0 : c0 + PASS]
            nc.sync.dma_start(out=raw, in_=rows.rearrange("(p j) c -> p j c", j=PACK))
            return raw

        def load_plane(queue, plane, rows, dram_rows):
            for q in range(4):
                queue.dma_start(out=plane[32 * q : 32 * q + rows].bitcast(I32), in_=dram_rows(slice(4 * q, 4 * q + 4)).bitcast(I32))

        RAW = [P, PACK, PASS]

        tab2_w = slot("slot_a", "tab2_w", [P, T2], I32)
        w4_w = slot("slot_b", "w4_w", [P, N], I32)
        w2_w = slot("slot_c", "w2_w", [P, 2, 2 * N], U8)
        tab_s = slot("slot_d", "tab_s", [P, T], U8)
        nc.vector.memset(tab_s[:].bitcast(I32), 0)
        nc.sync.dma_start(offs2_sb[:], offs2)
        nc.sync.dma_start(out=tab2_w[:], in_=as_words(tab2_words[0]))
        nc.sync.dma_start(out=w4_w[:], in_=as_words(w4_words[0]))
        nc.sync.dma_start(out=w2_w[:].bitcast(I32), in_=w2_words.rearrange("a p c -> p a c").bitcast(I32))
        nc.sync.dma_start(offs_sb[:], offs)
        nc.sync.dma_start(pos1_sb[:], pos1)
        w1_raw = {}
        for a, tag in enumerate(("slot_e", "slot_f")):
            w1_raw[(a, 0)] = load_weight(slot(tag, "w1_raw%d0" % a, RAW, F32)[:], w1, a, 0)
        load_plane(nc.sync, tab_s, 8, lambda r: tab_scales[:, r, :])

        def round_weight(raw, on_scalar):
            grouped = ring.tile([P, PACK * PASS], BF16, name="grouped", bufs=3, align_bytes=64)
            dst = grouped[:].rearrange("p (t m j) -> p m j t", t=PACK, j=PACK)
            src = raw.rearrange("p j (m t) -> p m j t", t=PACK)
            if on_scalar:
                nc.scalar.copy(out=dst, in_=src)
            else:
                nc.vector.tensor_copy(out=dst, in_=src)
            return grouped

        def quantise(name, grouped, cols):
            codes = held(name + "_codes", [P, cols], U32)
            scales = held(name + "_scales", [P, cols], U8)
            nc.vector.quantize_mx(out=codes[:].bitcast(FP8X4), scales=scales[:], in_=grouped[:])
            return codes, scales

        def weave(dst, src, on_scalar):
            dst = dst.rearrange("p (c i t) -> p c t i", t=PACK, i=4)
            src = src.rearrange("p t (c i) -> p c t i", i=4)
            if on_scalar:
                nc.scalar.copy(out=dst, in_=src)
            else:
                nc.vector.tensor_copy(out=dst, in_=src)

        def bank(tag):
            return psum.tile([P, BANK], F32, name=tag, bufs=3 if tag == "first" else 5)

        def cols(t, width=P):
            return slice(t * width, (t + 1) * width)

        v2_w = held("v2_w", [P, PICK], U32)
        v2_s = held("v2_s", [P, PICK], U8)
        w4d_w = held("w4d_w", [P, N], I32)
        w2d_w = held("w2d_w", [P, 2, PACK, 2 * P], U8)
        nc.vector.tensor_copy(out=v2_w[:], in_=tab2_w[:].bitcast(U32).indirect(offs2_sb[:]))
        tab_w = [slot("slot_a", "tab_w0", [P, T], I32)]
        nc.sync.dma_start(out=tab_w[0][:], in_=as_words(tab_words[0]))
        nc.vector.tensor_copy(out=w4d_w[:].rearrange("p (t m) -> p m t", t=PACK), in_=w4_w[:].rearrange("p (m t) -> p m t", t=PACK))
        tab2_s = slot("slot_b", "tab2_s", [P, T2], U8)
        nc.vector.memset(tab2_s[:].bitcast(I32), 0)
        load_plane(nc.sync, tab2_s, 4, lambda r: tab2_scales[0, r, :])
        nc.vector.tensor_copy(
            out=w2d_w[:].rearrange("p a t (m e) -> p a m t e", e=2),
            in_=w2_w[:].rearrange("p a (m t e) -> p a m t e", t=PACK, e=2),
        )
        affine = slot("slot_c", "affine", [P, 2, 2, PACK], F32)
        gain_sb, shift_sb = affine[:, 0], affine[:, 1]
        nc.sync.dma_start(out=gain_sb, in_=gain.rearrange("(b p t) -> p b t", b=2, t=PACK))
        nc.sync.dma_start(out=shift_sb, in_=shift.rearrange("(b p t) -> p b t", b=2, t=PACK))

        v_w = [held("v_w%d" % a, [P, S], U32) for a in range(2)]
        v_s = held("v_s", [P, S], U8)
        nc.vector.tensor_copy(out=v_s[:], in_=tab_s[:].indirect(offs_sb[:]))
        w1_q = {(0, 0): quantise("w1_00", round_weight(w1_raw[(0, 0)], True), PASS)}
        tab_w.append(slot("slot_e", "tab_w1", [P, T], I32))
        nc.sync.dma_start(out=tab_w[1][:], in_=as_words(tab_words[1]))
        w1_q[(1, 0)] = quantise("w1_10", round_weight(w1_raw[(1, 0)], True), PASS)
        late_raw = slot("slot_f", "late_raw", [P, 4, PACK, PASS], F32)
        for a in range(2):
            w1_raw[(a, 1)] = load_weight(late_raw[:, a], w1, a, PASS)
        w3_raw = [load_weight(late_raw[:, 2 + a], w3, a, 0) for a in range(2)]

        nc.vector.tensor_copy(out=v_w[0][:], in_=tab_w[0][:].bitcast(U32).indirect(offs_sb[:]))
        w_s = slot("slot_a", "w_s", [P, 3, N], U8)
        nc.vector.memset(w_s[:].rearrange("p a c -> p (a c)").bitcast(I32), 0)
        load_plane(nc.sync, w_s[:, 0:2], 4, lambda r: w2_scales[:, r, :].rearrange("a r c -> r a c"))
        load_plane(nc.sync, w_s[:, 2], 4, lambda r: w4_scales[0, r, :])
        nc.vector.tensor_copy(out=v2_s[:], in_=tab2_s[:].indirect(offs2_sb[:]))
        for half in range(2):
            nc.vector.tensor_copy(
                out=v_w[1][:, cols(half, BANK)],
                in_=tab_w[1][:].bitcast(U32).indirect(offs_sb[:, cols(half, BANK // 16)]),
            )

        def times_table(tag, weight, t, half):
            acc = bank(tag)
            for a in range(2):
                codes, scales = weight[a]
                nc.tensor.matmul_mx(
                    out=acc[:], lhsT=codes[:, cols(t)].bitcast(FP8X4), lhsT_scale=scales[:, cols(t)],
                    rhs=v_w[a][:, cols(half, BANK)].bitcast(FP8X4), rhs_scale=v_s[4 * a : P, cols(half, BANK)],
                    start=(a == 0), stop=(a == 1),
                )
            return acc

        def features(b, half):
            rounded = ring.tile([P, PACK, BANK], BF16, name="rounded", bufs=2, align_bytes=64)
            for t in range(PACK):
                acc = times_table("first", [w1_q[(0, b)], w1_q[(1, b)]], t, half)
                bent = ring.tile([P, BANK], F32, name="bent", bufs=6, align_bytes=64)
                nc.scalar.activation(out=bent[:], in_=acc[:], func=ACT.Tanh)
                gain_t, shift_t = gain_sb[:, b, t : t + 1], shift_sb[:, b, t : t + 1]
                if b != half:
                    nc.scalar.activation(out=rounded[:, t, :], in_=bent[:], func=ACT.Identity, scale=gain_t, bias=shift_t)
                else:
                    nc.vector.tensor_scalar(
                        out=rounded[:, t, :], in0=bent[:], scalar1=gain_t, scalar2=shift_t, op0=ALU.mult, op1=ALU.add
                    )
            woven = ring.tile([P, PACK * BANK], BF16, name="woven", bufs=2, align_bytes=64)
            weave(woven[:], rounded[:], (b, half) == (0, 0))
            return quantise("h_%d%d" % (b, half), woven, BANK)

        day = [held("day%d" % t, [P, S], F32) for t in range(PACK)]

        def straight(half):
            for t in range(PACK):
                acc = times_table("later", w3_q, t, half)
                nc.scalar.copy(out=day[t][:, cols(half, BANK)], in_=acc[:])

        def second_stage(half):
            for t in range(PACK):
                acc = bank("later")
                for b in range(2):
                    codes, scales = h_q[(b, half)]
                    nc.tensor.matmul_mx(
                        out=acc[:], lhsT=w2d_w[:, b, t, :].bitcast(FP4X4), lhsT_scale=wd_s[:, b, t, :],
                        rhs=codes[:].bitcast(FP8X4), rhs_scale=scales[:], start=(b == 0), stop=(b == 1),
                    )
                here = day[t][:, cols(half, BANK)]
                nc.vector.tensor_tensor(out=here, in0=acc[:], in1=here, op=ALU.max)

        h_q = {}
        h_q[(0, 0)] = features(0, 0)
        w1_q[(0, 1)] = quantise("w1_01", round_weight(w1_raw[(0, 1)], False), PASS)
        h_q[(0, 1)] = features(0, 1)
        w1_q[(1, 1)] = quantise("w1_11", round_weight(w1_raw[(1, 1)], False), PASS)
        h_q[(1, 0)] = features(1, 0)
        w3_q = [quantise("w3_%d" % a, round_weight(w3_raw[a], False), PASS) for a in range(2)]
        wd_s = slot("slot_f", "wd_s", [P, 3, PACK, P], U8)
        nc.vector.tensor_copy(
            out=wd_s[:].rearrange("p a t m -> p a m t"),
            in_=w_s[:].rearrange("p a (m t) -> p a m t", t=PACK),
        )
        h_q[(1, 1)] = features(1, 1)
        straight(0)
        second_stage(0)
        straight(1)
        second_stage(1)

        expo = []
        for t in range(PACK):
            acc = bank("first")
            nc.tensor.matmul_mx(
                out=acc[:], lhsT=w4d_w[:, cols(t)].bitcast(FP8X4), lhsT_scale=wd_s[:, 2, t, :],
                rhs=v2_w[:].bitcast(FP8X4), rhs_scale=v2_s[:], start=True, stop=True,
            )
            expo_t = held("expo%d" % t, [P, PICK], F32)
            nc.scalar.copy(out=expo_t[:], in_=acc[:])
            expo.append(expo_t)

        out_rows = out_0.rearrange("(p t) j -> p t j", t=PACK)
        out_words = as_words(out_1[0])
        y_codes = held("y_codes", [P, PICK], U32)
        y_scales = held("y_scales", [P, PICK], U8)
        for half, (j0, width) in enumerate(((0, 256), (256, 128), (384, 128))):
            js = slice(j0, j0 + width)
            y = held("y%d" % half, [P, PACK, width], F32)
            for t in range(PACK):
                nc.vector.tensor_tensor(
                    out=y[:, t, :], in0=day[t][:].indirect(pos1_sb[:, j0 // 16 : (j0 + width) // 16]), in1=expo[t][:, js], op=ALU.add
                )
            nc.sync.dma_start(out=out_rows[:, :, js], in_=y[:])
            y_woven = held("y_woven%d" % half, [P, PACK * width], BF16)
            weave(y_woven[:], y[:], half < 2)
            nc.vector.quantize_mx(out=y_codes[:, js].bitcast(FP8X4), scales=y_scales[:, js], in_=y_woven[:])
            nc.sync.dma_start(out=out_words[:, js], in_=y_codes[:, js].bitcast(I32))
        for q in range(4):
            queue = nc.scalar if q % 2 else nc.sync
            queue.dma_start(out=out_2[0, 4 * q : 4 * q + 4, :].bitcast(I32), in_=y_scales[32 * q : 32 * q + 4, :].bitcast(I32))
